import numpy as np
import ml_dtypes


def mxq(x, axis, fmt="e4m3"):
    dtype, down = {"e4m3": (ml_dtypes.float8_e4m3fn, 7), "e5m2": (ml_dtypes.float8_e5m2, 14)}[fmt]
    v = np.moveaxis(np.asarray(x, np.float32).astype(ml_dtypes.bfloat16).astype(np.float64), axis, -1)
    blocks = v.reshape(v.shape[:-1] + (-1, 32))
    amax = np.abs(blocks).max(-1, keepdims=True)
    byte = np.maximum(np.where(amax > 0, np.frexp(amax)[1] - 1 + 127, 0) - down, 1)
    scale = np.exp2(byte - 127.0)
    codes = (blocks / scale).astype(np.float32).astype(dtype).astype(np.float64)
    return np.moveaxis((codes * scale).reshape(v.shape), -1, axis)


WIDE = False


def mx_kscale(k):
    if not WIDE:
        return np.ones(k)
    levels = np.array([10, -10, 5, -5, 0])
    if k % 512:
        return np.exp2(np.random.permutation(np.resize(levels, k // 32))).repeat(32)
    a = np.empty((k // 512, 16))
    for p in range(k // 512):
        a[p, :8] = np.random.permutation(np.resize(levels, 8))
        for g in range(8):
            far = levels[np.abs(levels - a[p, g]) >= 10]
            a[p, g + 8] = far[np.random.randint(len(far))]
    return np.exp2(a.ravel()).repeat(32)


def f64(x):
    return np.asarray(x).astype(np.float64)


def striped8(idx):
    return np.concatenate([x.reshape(-1, 16).T for x in idx]).astype(np.uint16)


def runs(offs, k):
    lists = np.stack([offs[16 * r : 16 * r + 16].T.reshape(-1) for r in range(8)]).astype(np.int64)
    return lists[np.arange(k) % 512 // 64]


def pack_weight(w):
    k, n = w.shape
    w = f64(np.asarray(w, np.float32).astype(ml_dtypes.bfloat16)).reshape(k // 32, 32, n)
    amax = np.abs(w).max(1)
    byte = np.clip(np.where(amax > 0, np.frexp(amax)[1] - 1 + 127 - 7, 1), 1, 254)
    scaled = (w * np.exp2(127.0 - byte)[:, None, :]).reshape(k, n).astype(np.float32)
    words = np.ascontiguousarray(scaled.reshape(k // 512, 128, 4, n).transpose(0, 1, 3, 2)).astype(ml_dtypes.float8_e4m3fn).view(np.uint8)
    return words, np.ascontiguousarray(byte.astype(np.uint8).reshape(k // 512, 16, n))


def unpack_weight(words, scales):
    g, p, n, _ = words.shape
    vals = np.ascontiguousarray(words).view(ml_dtypes.float8_e4m3fn).astype(np.float64) * np.repeat(np.exp2(scales.astype(np.float64) - 127.0), 8, axis=1)[..., None]
    return vals.transpose(0, 1, 3, 2).reshape(g * 512, n)


def sigmoid(v):
    return 1.0 / (1.0 + np.exp(-np.maximum(v, -700.0)))


K, T, S, N, H, W = 512, 2048, 512, 512, 512, 256


def setup_inputs():
    n = np.random.standard_normal
    s = mx_kscale(K)[:, None]
    u = mx_kscale(H)
    packed_xT = pack_weight(n((K, T)) * s)
    perm = np.stack([np.random.permutation(S) for _ in range(8)])
    return {
        "x_words": packed_xT[0],
        "x_scales": packed_xT[1],
        "w1": (n((K, H)) / np.sqrt(K) / s).astype(np.float32),
        "sl": np.random.uniform(1.5, 3.0, (H, 1)).astype(np.float32),
        "th": (0.5 * n((H, 1))).astype(np.float32),
        "gn": (np.random.uniform(0.5, 1.5, (H, 1)) * u[:, None]).astype(np.float32),
        "w2": (n((H, N)) / np.sqrt(H) / u[:, None]).astype(np.float32),
        "offs": striped8(np.random.randint(0, T, (8, S))),
        "n1": striped8(np.stack([np.random.permutation(S) for _ in range(8)])),
        "n2": striped8(np.stack([np.random.permutation(S) for _ in range(8)])),
        "n3": striped8(perm[:, :W]),
        "n4": striped8(perm[:, W:]),
        "n5": striped8(np.stack([np.random.permutation(S) for _ in range(8)])),
    }


def reference(x_words, x_scales, w1, sl, th, gn, w2, offs, n1, n2, n3, n4, n5):
    xq = unpack_weight(x_words, x_scales)[np.arange(K)[:, None], runs(offs, K)]
    y = mxq(f64(w1), 0, "e4m3").T @ xq
    sg = sigmoid(f64(sl) * (y[np.arange(H)[:, None], runs(n1, H)] - f64(th)))
    z = f64(gn) * (1.5 * (y * (sg - (sg[np.arange(H)[:, None], runs(n2, H)]))))
    h = mxq(f64(w2), 0, "e4m3").T @ mxq(z, 0, "e4m3")
    pa = h[np.arange(N)[:, None], runs(n3, N)]
    pb = h[np.arange(N)[:, None], runs(n4, N)]
    rb = pa - pb
    ra = pa + pb
    ds = np.zeros((N, S))
    ds[np.arange(N)[:, None], runs(n3, N)] = ra
    dt = ds.copy()
    dt[np.arange(N)[:, None], runs(n4, N)] = rb
    return np.maximum(dt, dt[np.arange(N)[:, None], runs(n5, N)])

@@ -1,0 +1,227 @@
+from contextlib import ExitStack
+
+import concourse.mybir as mybir
+
+F32 = mybir.dt.float32
+BF16 = mybir.dt.bfloat16
+I32 = mybir.dt.int32
+U32 = mybir.dt.uint32
+U16 = mybir.dt.uint16
+U8 = mybir.dt.uint8
+FP8X4 = mybir.dt.float8_e4m3fn_x4
+ALU = mybir.AluOpType
+ACT = mybir.ActivationFunctionType
+
+P = 128
+PACK = 4
+K, T, S, H, N, W = 512, 2048, 512, 512, 512, 256
+HALF = S // 2
+FLOPS = 2 * K * H * S + 2 * H * N * S
+
+
+def tile_picked_hashedbhaarh_none_p_kernel(
+    tc, x_words, x_scales, w1, sl, th, gn, w2, offs, n1, n2, n3, n4, n5, out
+):
+    nc = tc.nc
+    with ExitStack() as ctx:
+        lists = ctx.enter_context(tc.tile_pool(name="lists", bufs=1))
+        keep = ctx.enter_context(tc.tile_pool(name="keep", bufs=1))
+        psum = ctx.enter_context(tc.psum_pool(name="psum", bufs=1))
+
+        def load_list(src, name):
+            t = lists.tile(list(src.shape), U16, name=name)
+            nc.sync.dma_start(t[:], src)
+            return t
+
+        def cols(h):
+            return slice(h * HALF, (h + 1) * HALF)
+
+        def entries(lst, h):
+            return lst[:, h * HALF // 16 : (h + 1) * HALF // 16]
+
+        def load_weight_half(w, h, name):
+            raw = keep.tile([P, PACK, HALF], F32, name=name)
+            nc.sync.dma_start(raw[:], w.rearrange("(p j) c -> p j c", j=PACK)[:, :, cols(h)])
+            return raw
+
+        def deal(engine_copy, grouped, raw, h, lo, hi):
+            m0 = h * HALF // PACK
+            engine_copy(
+                grouped[:, :, m0 + lo : m0 + hi, :].rearrange("p t m j -> p m j t"),
+                raw.rearrange("p j (m t) -> p m j t", t=PACK)[:, lo:hi],
+            )
+
+        def quantize(src, width, name):
+            codes = keep.tile([P, width], U32, name=name + "_codes", align_bytes=64)
+            scales = keep.tile([P, width], U8, name=name + "_scales", align_bytes=64)
+            nc.vector.quantize_mx(out=codes[:].bitcast(FP8X4), scales=scales[:], in_=src)
+            return codes, scales
+
+        scale_table = keep.tile([P, T], U8, name="scale_table")
+        nc.gpsimd.memset(scale_table[:].bitcast(I32), 0)
+        x_plane = keep.tile([P, S], U8, name="x_plane", align_bytes=64)
+        nc.gpsimd.memset(x_plane[:].bitcast(I32), 0)
+        offs_t = load_list(offs, "offs_t")
+        nc.sync.dma_start(scale_table[0:P:8, :].bitcast(I32), x_scales[0].bitcast(I32))
+        sl_t = keep.tile([P, PACK], F32, name="sl_t")
+        th_t = keep.tile([P, PACK], F32, name="th_t")
+        gn_t = keep.tile([P, PACK], F32, name="gn_t")
+
+        def load_rows(dst, src):
+            nc.sync.dma_start(dst[:], src.rearrange("(p t) o -> p (t o)", t=PACK))
+
+        def load_half(raw, w, h):
+            nc.sync.dma_start(raw[:, h], w.rearrange("(p j) c -> p j c", j=PACK)[:, :, cols(h)])
+
+        w1_all = keep.tile([P, 2, PACK, HALF], F32, name="w1_raw", tag="raw")
+        load_half(w1_all, w1, 0)
+        n1_t = load_list(n1, "n1_t")
+        load_rows(sl_t, sl)
+        load_rows(th_t, th)
+        load_half(w1_all, w1, 1)
+        word_table = keep.tile([P, T], I32, name="word_table")
+        nc.sync.dma_start(word_table[:], x_words[0].rearrange("p n r -> p (n r)").bitcast(I32))
+
+        w1_grouped = keep.tile([P, PACK, P, PACK], BF16, name="w1_grouped", align_bytes=64)
+        deal(nc.scalar.copy, w1_grouped, w1_all[:, 0], 0, 0, 64)
+        picked_scales = keep.tile([P, S], U8, name="picked_scales")
+        nc.vector.tensor_copy(picked_scales[:], scale_table[:].indirect(offs_t[:]))
+        for j in range(4):
+            nc.scalar.dma_start(
+                x_plane[j:P:32, :].bitcast(I32),
+                picked_scales[8 * j : P : 32, :].bitcast(I32),
+            )
+        deal(nc.vector.tensor_copy, w1_grouped, w1_all[:, 1], 1, 0, 64)
+        w1_q = [quantize(w1_grouped[:, t].rearrange("p m j -> p (m j)"), P, "w1_%d" % t) for t in range(PACK)]
+
+        load_rows(gn_t, gn)
+        n2_t = load_list(n2, "n2_t")
+        w2_all = keep.tile([P, 2, PACK, HALF], F32, name="w2_raw", tag="raw")
+        for h in range(2):
+            load_half(w2_all, w2, h)
+        w2_raw = [w2_all[:, h] for h in range(2)]
+        n3_t = load_list(n3, "n3_t")
+        n4_t = load_list(n4, "n4_t")
+        n5_t = load_list(n5, "n5_t")
+
+        bias_t = keep.tile([P, PACK], F32, name="bias_t")
+        nc.vector.scalar_tensor_tensor(bias_t[:], sl_t[:], -1.0, th_t[:], ALU.mult, ALU.mult)
+        gain_t = keep.tile([P, PACK], F32, name="gain_t")
+        nc.vector.tensor_scalar(gain_t[:], gn_t[:], -1.5, None, ALU.mult)
+
+        y_ps = {}
+        for h in range(2):
+            picked = keep.tile([P, HALF], U32, name="picked_words%d" % h, align_bytes=64)
+            nc.vector.tensor_copy(picked[:], word_table[:].bitcast(U32).indirect(entries(offs_t, h)))
+            for t in range(PACK):
+                y_ps[t, h] = psum.tile([P, HALF], F32, name="y_ps%d%d" % (t, h), tag="bank%d%d" % (t, h))
+                nc.tensor.matmul_mx(
+                    out=y_ps[t, h][:],
+                    lhsT=w1_q[t][0][:].bitcast(FP8X4),
+                    lhsT_scale=w1_q[t][1][:],
+                    rhs=picked[:].bitcast(FP8X4),
+                    rhs_scale=x_plane[:, cols(h)],
+                    start=True,
+                    stop=True,
+                )
+        y = [keep.tile([P, S], F32, name="y%d" % t) for t in range(PACK)]
+        sg = [keep.tile([P, S], F32, name="sg%d" % t) for t in range(PACK)]
+        for t in range(PACK):
+            for h in range(2):
+                nc.vector.tensor_copy(y[t][:, cols(h)], y_ps[t, h][:])
+            for h in range(2):
+                nc.scalar.activation(
+                    out=sg[t][:, cols(h)],
+                    in_=y[t][:].indirect(entries(n1_t, h)),
+                    func=ACT.Sigmoid,
+                    scale=sl_t[:, t : t + 1],
+                    bias=bias_t[:, t : t + 1],
+                )
+
+        z_planes = [keep.tile([P, PACK, HALF], BF16, name="z_planes%d" % h) for h in range(2)]
+
+        def gate(t, h, other):
+            diff = keep.tile([P, HALF], F32, name="diff%d%d" % (t, h))
+            if other is None:
+                fetched = keep.tile([P, HALF], F32, name="fetched%d%d" % (t, h))
+                nc.scalar.activation(out=fetched[:], in_=sg[t][:].indirect(entries(n2_t, h)), func=ACT.Copy)
+                nc.vector.tensor_tensor(diff[:], fetched[:], sg[t][:, cols(h)], ALU.subtract)
+            else:
+                nc.vector.tensor_tensor(diff[:], sg[t][:].indirect(entries(n2_t, h)), other[:, cols(h)], ALU.subtract)
+            nc.vector.scalar_tensor_tensor(
+                z_planes[h][:, t, :], diff[:], gain_t[:, t : t + 1], y[t][:, cols(h)], ALU.mult, ALU.mult
+            )
+
+        for t in range(2):
+            twin = keep.tile([P, S], F32, name="sg_twin%d" % t)
+            nc.vector.tensor_copy(twin[:], sg[t][:])
+            for h in range(2):
+                gate(t, h, twin)
+
+        w2_grouped = keep.tile([P, PACK, P, PACK], BF16, name="w2_grouped", align_bytes=64)
+        z_q = []
+        for h in range(2):
+            for t in range(2, PACK):
+                gate(t, h, None)
+            z_grouped = keep.tile([P, HALF, PACK], BF16, name="z_grouped%d" % h, align_bytes=64)
+            copy = nc.scalar.copy if h == 0 else nc.vector.tensor_copy
+            copy(
+                z_grouped[:].rearrange("p (c i) t -> p c t i", i=4),
+                z_planes[h][:].rearrange("p t (c i) -> p c t i", i=4),
+            )
+            z_q.append(quantize(z_grouped[:].rearrange("p s t -> p (s t)"), HALF, "z_%d" % h))
+            deal(nc.scalar.copy if h == 1 else nc.vector.tensor_copy, w2_grouped, w2_raw[h], h, 0, 64)
+        w2_q = [quantize(w2_grouped[:, t].rearrange("p m j -> p (m j)"), P, "w2_%d" % t) for t in range(PACK)]
+
+        out_rows = out.rearrange("(p t) s -> p t s", t=PACK)
+        hid, pa, pb, nb, dt = {}, {}, {}, {}, {}
+
+        def product(t):
+            hid[t] = keep.tile([P, S], F32, name="hid%d" % t)
+            for h in range(2):
+                ps = psum.tile([P, HALF], F32, name="h_ps%d%d" % (t, h), tag="bank%d%d" % (t, h))
+                nc.tensor.matmul_mx(
+                    out=ps[:],
+                    lhsT=w2_q[t][0][:].bitcast(FP8X4),
+                    lhsT_scale=w2_q[t][1][:],
+                    rhs=z_q[h][0][:].bitcast(FP8X4),
+                    rhs_scale=z_q[h][1][:],
+                    start=True,
+                    stop=True,
+                )
+                nc.scalar.copy(hid[t][:, cols(h)], ps[:])
+
+        def pair(t):
+            pa[t] = keep.tile([P, W], F32, name="pa%d" % t)
+            pb[t] = keep.tile([P, W], F32, name="pb%d" % t)
+            nb[t] = keep.tile([P, W], F32, name="nb%d" % t)
+            nc.scalar.activation(out=pa[t][:], in_=hid[t][:].indirect(n3_t[:]), func=ACT.Copy)
+            if t == 0:
+                nc.vector.tensor_copy(pb[t][:], hid[t][:].indirect(n4_t[:]))
+            else:
+                nc.scalar.activation(out=pb[t][:], in_=hid[t][:].indirect(n4_t[:]), func=ACT.Copy)
+            nc.scalar.activation(out=nb[t][:], in_=pb[t][:], func=ACT.Copy, scale=-1.0)
+
+        def put(t):
+            dt[t] = keep.tile([P, S], F32, name="dt%d" % t)
+            nc.vector.tensor_tensor(dt[t][:].indirect(n3_t[:]), pa[t][:], pb[t][:], ALU.add)
+            nc.vector.tensor_tensor(dt[t][:].indirect(n4_t[:]), pa[t][:], nb[t][:], ALU.add)
+
+        def finish(t):
+            for h in range(2):
+                far = keep.tile([P, HALF], F32, name="far%d%d" % (t, h))
+                nc.scalar.activation(out=far[:], in_=dt[t][:].indirect(entries(n5_t, h)), func=ACT.Copy)
+                res = keep.tile([P, HALF], F32, name="res%d%d" % (t, h))
+                nc.vector.tensor_tensor(res[:], far[:], dt[t][:, cols(h)], ALU.max)
+                nc.sync.dma_start(out_rows[:, t, cols(h)], res[:])
+
+        product(0)
+        pair(0)
+        for t in range(PACK):
+            if t + 1 < PACK:
+                product(t + 1)
+                pair(t + 1)
+            put(t)
+            if t > 0:
+                finish(t - 1)
+        finish(PACK - 1)

@@ -17,6 +17,8 @@ PACK = 4
 K, T, S, H, N, W = 512, 2048, 512, 512, 512, 256
 HALF = S // 2
 FLOPS = 2 * K * H * S + 2 * H * N * S
+CHUNKS = [slice(0, 256), slice(256, 384), slice(384, 512)]
+OWN = 2
 
 
 def tile_picked_hashedbhaarh_none_p_kernel(
@@ -36,192 +38,214 @@ def tile_picked_hashedbhaarh_none_p_kernel(
         def cols(h):
             return slice(h * HALF, (h + 1) * HALF)
 
-        def entries(lst, h):
-            return lst[:, h * HALF // 16 : (h + 1) * HALF // 16]
+        def entries(lst, span):
+            return lst[:, span.start // 16 : span.stop // 16]
 
-        def load_weight_half(w, h, name):
-            raw = keep.tile([P, PACK, HALF], F32, name=name)
+        def load_half(w, h, name, tag):
+            raw = keep.tile([P, PACK, HALF], F32, name=name, tag=tag)
             nc.sync.dma_start(raw[:], w.rearrange("(p j) c -> p j c", j=PACK)[:, :, cols(h)])
             return raw
 
-        def deal(engine_copy, grouped, raw, h, lo, hi):
-            m0 = h * HALF // PACK
+        def deal(engine_copy, grouped, raw, h):
             engine_copy(
-                grouped[:, :, m0 + lo : m0 + hi, :].rearrange("p t m j -> p m j t"),
-                raw.rearrange("p j (m t) -> p m j t", t=PACK)[:, lo:hi],
+                grouped[:, :, h * 64 : (h + 1) * 64, :].rearrange("p t m j -> p m j t"),
+                raw[:].rearrange("p j (m t) -> p m j t", t=PACK),
             )
 
-        def quantize(src, width, name):
-            codes = keep.tile([P, width], U32, name=name + "_codes", align_bytes=64)
+        def quantize(grouped, t0, t1, name, tag=None):
+            width = (t1 - t0) * P
+            codes = keep.tile([P, width], U32, name=name + "_codes", tag=tag or name, align_bytes=64)
             scales = keep.tile([P, width], U8, name=name + "_scales", align_bytes=64)
-            nc.vector.quantize_mx(out=codes[:].bitcast(FP8X4), scales=scales[:], in_=src)
-            return codes, scales
+            nc.vector.quantize_mx(
+                out=codes[:].bitcast(FP8X4), scales=scales[:], in_=grouped[:, t0:t1].rearrange("p t m j -> p (t m j)")
+            )
+            return [(codes[:, i * P : (i + 1) * P], scales[:, i * P : (i + 1) * P]) for i in range(t1 - t0)]
+
+        def product(weights, moving, moving_scales, span, tag):
+            ps = psum.tile([P, span.stop - span.start], F32, name="ps_" + tag, tag=tag)
+            nc.tensor.matmul_mx(
+                out=ps[:],
+                lhsT=weights[0].bitcast(FP8X4),
+                lhsT_scale=weights[1],
+                rhs=moving[:, span].bitcast(FP8X4),
+                rhs_scale=moving_scales[:, span],
+                start=True,
+                stop=True,
+            )
+            return ps
+
+        def fetch(dst, window, offsets):
+            nc.scalar.activation(out=dst, in_=window[:].indirect(offsets), func=ACT.Copy)
+
+        whole = slice(0, S)
 
         scale_table = keep.tile([P, T], U8, name="scale_table")
         nc.gpsimd.memset(scale_table[:].bitcast(I32), 0)
-        x_plane = keep.tile([P, S], U8, name="x_plane", align_bytes=64)
-        nc.gpsimd.memset(x_plane[:].bitcast(I32), 0)
         offs_t = load_list(offs, "offs_t")
-        nc.sync.dma_start(scale_table[0:P:8, :].bitcast(I32), x_scales[0].bitcast(I32))
+        for e in range(2):
+            nc.sync.dma_start(scale_table[e:P:16, :].bitcast(I32), x_scales[0, e:16:2].bitcast(I32))
+        w1_raw = [load_half(w1, 0, "w1_raw0", "raw_a")]
+        n1_t = load_list(n1, "n1_t")
+        n2_t = load_list(n2, "n2_t")
+        n3_t = load_list(n3, "n3_t")
+        w1_raw.append(load_half(w1, 1, "w1_raw1", "raw_b"))
+        word_table = keep.tile([P, T], I32, name="word_table")
+        nc.sync.dma_start(word_table[:], x_words[0].rearrange("p n r -> p (n r)").bitcast(I32))
+        w2_raw = [load_half(w2, h, "w2_raw%d" % h, "raw_%s" % "cb"[h]) for h in range(1)]
+        n4_t = load_list(n4, "n4_t")
+        n5_t = load_list(n5, "n5_t")
         sl_t = keep.tile([P, PACK], F32, name="sl_t")
         th_t = keep.tile([P, PACK], F32, name="th_t")
         gn_t = keep.tile([P, PACK], F32, name="gn_t")
-
-        def load_rows(dst, src):
-            nc.sync.dma_start(dst[:], src.rearrange("(p t) o -> p (t o)", t=PACK))
-
-        def load_half(raw, w, h):
-            nc.sync.dma_start(raw[:, h], w.rearrange("(p j) c -> p j c", j=PACK)[:, :, cols(h)])
-
-        w1_all = keep.tile([P, 2, PACK, HALF], F32, name="w1_raw", tag="raw")
-        load_half(w1_all, w1, 0)
-        n1_t = load_list(n1, "n1_t")
-        load_rows(sl_t, sl)
-        load_rows(th_t, th)
-        load_half(w1_all, w1, 1)
-        word_table = keep.tile([P, T], I32, name="word_table")
-        nc.sync.dma_start(word_table[:], x_words[0].rearrange("p n r -> p (n r)").bitcast(I32))
+        for dst, src in ((sl_t, sl), (th_t, th), (gn_t, gn)):
+            nc.gpsimd.dma_start(dst[:], src.rearrange("(p t) o -> p (t o)", t=PACK))
 
         w1_grouped = keep.tile([P, PACK, P, PACK], BF16, name="w1_grouped", align_bytes=64)
-        deal(nc.scalar.copy, w1_grouped, w1_all[:, 0], 0, 0, 64)
+        deal(nc.scalar.copy, w1_grouped, w1_raw[0], 0)
         picked_scales = keep.tile([P, S], U8, name="picked_scales")
         nc.vector.tensor_copy(picked_scales[:], scale_table[:].indirect(offs_t[:]))
-        for j in range(4):
+        x_plane = keep.tile([P, S], U8, name="x_plane", align_bytes=64)
+        nc.vector.tensor_copy(x_plane[:].bitcast(I32), picked_scales[:].bitcast(I32))
+        for e in range(2):
             nc.scalar.dma_start(
-                x_plane[j:P:32, :].bitcast(I32),
-                picked_scales[8 * j : P : 32, :].bitcast(I32),
+                x_plane[2 + e : P : 32, :].bitcast(I32),
+                picked_scales[16 + e : P : 32, :].bitcast(I32),
             )
-        deal(nc.vector.tensor_copy, w1_grouped, w1_all[:, 1], 1, 0, 64)
-        w1_q = [quantize(w1_grouped[:, t].rearrange("p m j -> p (m j)"), P, "w1_%d" % t) for t in range(PACK)]
-
-        load_rows(gn_t, gn)
-        n2_t = load_list(n2, "n2_t")
-        w2_all = keep.tile([P, 2, PACK, HALF], F32, name="w2_raw", tag="raw")
-        for h in range(2):
-            load_half(w2_all, w2, h)
-        w2_raw = [w2_all[:, h] for h in range(2)]
-        n3_t = load_list(n3, "n3_t")
-        n4_t = load_list(n4, "n4_t")
-        n5_t = load_list(n5, "n5_t")
+        deal(nc.vector.tensor_copy, w1_grouped, w1_raw[1], 1)
+        w1_ops = quantize(w1_grouped, 0, 1, "w1_first") + quantize(w1_grouped, 1, PACK, "w1_rest")
+        w2_raw.append(load_half(w2, 1, "w2_raw1", "raw_b"))
 
         bias_t = keep.tile([P, PACK], F32, name="bias_t")
         nc.vector.scalar_tensor_tensor(bias_t[:], sl_t[:], -1.0, th_t[:], ALU.mult, ALU.mult)
         gain_t = keep.tile([P, PACK], F32, name="gain_t")
         nc.vector.tensor_scalar(gain_t[:], gn_t[:], -1.5, None, ALU.mult)
 
-        y_ps = {}
-        for h in range(2):
-            picked = keep.tile([P, HALF], U32, name="picked_words%d" % h, align_bytes=64)
-            nc.vector.tensor_copy(picked[:], word_table[:].bitcast(U32).indirect(entries(offs_t, h)))
-            for t in range(PACK):
-                y_ps[t, h] = psum.tile([P, HALF], F32, name="y_ps%d%d" % (t, h), tag="bank%d%d" % (t, h))
-                nc.tensor.matmul_mx(
-                    out=y_ps[t, h][:],
-                    lhsT=w1_q[t][0][:].bitcast(FP8X4),
-                    lhsT_scale=w1_q[t][1][:],
-                    rhs=picked[:].bitcast(FP8X4),
-                    rhs_scale=x_plane[:, cols(h)],
-                    start=True,
-                    stop=True,
-                )
+        picked = keep.tile([P, S], U32, name="picked_words", align_bytes=64)
         y = [keep.tile([P, S], F32, name="y%d" % t) for t in range(PACK)]
         sg = [keep.tile([P, S], F32, name="sg%d" % t) for t in range(PACK)]
+        for h in range(2):
+            nc.vector.tensor_copy(picked[:, cols(h)], word_table[:].bitcast(U32).indirect(entries(offs_t, cols(h))))
         for t in range(PACK):
             for h in range(2):
-                nc.vector.tensor_copy(y[t][:, cols(h)], y_ps[t, h][:])
+                ps = product(w1_ops[t], picked, x_plane, cols(h), "bank%d" % (2 * t + h))
+                [[nc.scalar.copy, nc.scalar.copy, nc.scalar.copy, nc.vector.tensor_copy], [nc.vector.tensor_copy, nc.vector.tensor_copy, nc.vector.tensor_copy, nc.vector.tensor_copy]][h][t](y[t][:, cols(h)], ps[:])
+        w2_grouped = keep.tile([P, PACK, P, PACK], BF16, name="w2_grouped", align_bytes=64)
+        for t in range(PACK):
             for h in range(2):
                 nc.scalar.activation(
                     out=sg[t][:, cols(h)],
-                    in_=y[t][:].indirect(entries(n1_t, h)),
+                    in_=y[t][:].indirect(entries(n1_t, cols(h))),
                     func=ACT.Sigmoid,
                     scale=sl_t[:, t : t + 1],
                     bias=bias_t[:, t : t + 1],
                 )
 
-        z_planes = [keep.tile([P, PACK, HALF], BF16, name="z_planes%d" % h) for h in range(2)]
+        z_head = keep.tile([P, PACK, HALF], BF16, name="z_head")
+        z_tail = keep.tile([P, 2, PACK, HALF // 2], BF16, name="z_tail")
+        z_planes = [z_head[:], z_tail[:, 0], z_tail[:, 1]]
+        diff = [keep.tile([P, S], F32, name="diff%d" % t) for t in range(PACK)]
 
-        def gate(t, h, other):
-            diff = keep.tile([P, HALF], F32, name="diff%d%d" % (t, h))
-            if other is None:
-                fetched = keep.tile([P, HALF], F32, name="fetched%d%d" % (t, h))
-                nc.scalar.activation(out=fetched[:], in_=sg[t][:].indirect(entries(n2_t, h)), func=ACT.Copy)
-                nc.vector.tensor_tensor(diff[:], fetched[:], sg[t][:, cols(h)], ALU.subtract)
-            else:
-                nc.vector.tensor_tensor(diff[:], sg[t][:].indirect(entries(n2_t, h)), other[:, cols(h)], ALU.subtract)
-            nc.vector.scalar_tensor_tensor(
-                z_planes[h][:, t, :], diff[:], gain_t[:, t : t + 1], y[t][:, cols(h)], ALU.mult, ALU.mult
-            )
+        def scale_diff(dst, t, c, pattern=None):
+            d, v = diff[t][:, c], y[t][:, c]
+            if pattern:
+                d, v = d.rearrange(pattern, u=2), v.rearrange(pattern, u=2)
+            nc.vector.scalar_tensor_tensor(dst, d, gain_t[:, t : t + 1], v, ALU.mult, ALU.mult)
 
-        for t in range(2):
-            twin = keep.tile([P, S], F32, name="sg_twin%d" % t)
+
+        def copy_of(t):
+            twin = keep.tile([P, S], F32, name="sg_twin%d" % t, tag="twin")
             nc.vector.tensor_copy(twin[:], sg[t][:])
+            return twin
+
+        twin = copy_of(0)
+        deal(nc.vector.tensor_copy, w2_grouped, w2_raw[0], 0)
+        deal(nc.vector.tensor_copy, w2_grouped, w2_raw[1], 1)
+        w2_ops = quantize(w2_grouped, 0, 1, "w2_first")
+        for t in range(OWN):
             for h in range(2):
-                gate(t, h, twin)
-
-        w2_grouped = keep.tile([P, PACK, P, PACK], BF16, name="w2_grouped", align_bytes=64)
-        z_q = []
-        for h in range(2):
-            for t in range(2, PACK):
-                gate(t, h, None)
-            z_grouped = keep.tile([P, HALF, PACK], BF16, name="z_grouped%d" % h, align_bytes=64)
-            copy = nc.scalar.copy if h == 0 else nc.vector.tensor_copy
-            copy(
-                z_grouped[:].rearrange("p (c i) t -> p c t i", i=4),
-                z_planes[h][:].rearrange("p t (c i) -> p c t i", i=4),
-            )
-            z_q.append(quantize(z_grouped[:].rearrange("p s t -> p (s t)"), HALF, "z_%d" % h))
-            deal(nc.scalar.copy if h == 1 else nc.vector.tensor_copy, w2_grouped, w2_raw[h], h, 0, 64)
-        w2_q = [quantize(w2_grouped[:, t].rearrange("p m j -> p (m j)"), P, "w2_%d" % t) for t in range(PACK)]
-
-        out_rows = out.rearrange("(p t) s -> p t s", t=PACK)
-        hid, pa, pb, nb, dt = {}, {}, {}, {}, {}
-
-        def product(t):
-            hid[t] = keep.tile([P, S], F32, name="hid%d" % t)
-            for h in range(2):
-                ps = psum.tile([P, HALF], F32, name="h_ps%d%d" % (t, h), tag="bank%d%d" % (t, h))
-                nc.tensor.matmul_mx(
-                    out=ps[:],
-                    lhsT=w2_q[t][0][:].bitcast(FP8X4),
-                    lhsT_scale=w2_q[t][1][:],
-                    rhs=z_q[h][0][:].bitcast(FP8X4),
-                    rhs_scale=z_q[h][1][:],
-                    start=True,
-                    stop=True,
+                nc.vector.tensor_tensor(
+                    diff[t][:, cols(h)], sg[t][:].indirect(entries(n2_t, cols(h))), twin[:, cols(h)], ALU.subtract
                 )
-                nc.scalar.copy(hid[t][:, cols(h)], ps[:])
+            if t + 1 < OWN:
+                twin = copy_of(t + 1)
+            scale_diff(z_head[:, t, :], t, cols(0))
+            scale_diff(z_tail[:, :, t, :], t, cols(1), "p (u c) -> p u c")
+        z_codes = keep.tile([P, S], U32, name="z_codes", align_bytes=64)
+        z_scales = keep.tile([P, S], U8, name="z_scales", align_bytes=64)
+        fetched = {t: keep.tile([P, S], F32, name="fetched%d" % t) for t in range(OWN, PACK)}
+        z_grouped = keep.tile([P, S, PACK], BF16, name="z_grouped", tag="late", align_bytes=64)
 
-        def pair(t):
-            pa[t] = keep.tile([P, W], F32, name="pa%d" % t)
-            pb[t] = keep.tile([P, W], F32, name="pb%d" % t)
-            nb[t] = keep.tile([P, W], F32, name="nb%d" % t)
-            nc.scalar.activation(out=pa[t][:], in_=hid[t][:].indirect(n3_t[:]), func=ACT.Copy)
-            if t == 0:
-                nc.vector.tensor_copy(pb[t][:], hid[t][:].indirect(n4_t[:]))
-            else:
-                nc.scalar.activation(out=pb[t][:], in_=hid[t][:].indirect(n4_t[:]), func=ACT.Copy)
+        def quantize_z(c):
+            nc.vector.quantize_mx(
+                out=z_codes[:, c].bitcast(FP8X4), scales=z_scales[:, c], in_=z_grouped[:, c].rearrange("p s t -> p (s t)")
+            )
+
+        for i, c in enumerate(CHUNKS):
+            for t in range(OWN, PACK):
+                fetch(fetched[t][:, c], sg[t], entries(n2_t, c))
+                nc.vector.tensor_tensor(diff[t][:, c], fetched[t][:, c], sg[t][:, c], ALU.subtract)
+            for t in range(OWN, PACK):
+                scale_diff(z_planes[i][:, t, :], t, c)
+
+            if i == 2:
+                quantize_z(CHUNKS[0])
+            [nc.scalar.copy, nc.scalar.copy, nc.vector.tensor_copy][i](
+                z_grouped[:, c].rearrange("p (c i) t -> p c t i", i=4),
+                z_planes[i].rearrange("p t (c i) -> p c t i", i=4),
+            )
+        for c in CHUNKS[1:]:
+            quantize_z(c)
+
+
+        w2_ops = w2_ops + quantize(w2_grouped, 1, PACK, "w2_rest", "late")
+        out_rows = out.rearrange("(p t) s -> p t s", t=PACK)
+        hid = [keep.tile([P, S], F32, name="hid%d" % t) for t in range(PACK)]
+        pa = [keep.tile([P, W], F32, name="pa%d" % t) for t in range(PACK)]
+        pb = [keep.tile([P, W], F32, name="pb%d" % t) for t in range(PACK)]
+        nb = [keep.tile([P, W], F32, name="nb%d" % t) for t in range(PACK)]
+        dt = [keep.tile([P, S], F32, name="dt%d" % t) for t in range(PACK)]
+        far = [keep.tile([P, S], F32, name="far%d" % t) for t in range(PACK)]
+        res = [keep.tile([P, S], F32, name="res%d" % t) for t in range(PACK)]
+
+        def put_sum(t, span):
+            nc.vector.tensor_tensor(dt[t][:].indirect(entries(n3_t, span)), pa[t][:, span], pb[t][:, span], ALU.add)
+
+        def put_difference(t):
             nc.scalar.activation(out=nb[t][:], in_=pb[t][:], func=ACT.Copy, scale=-1.0)
-
-        def put(t):
-            dt[t] = keep.tile([P, S], F32, name="dt%d" % t)
-            nc.vector.tensor_tensor(dt[t][:].indirect(n3_t[:]), pa[t][:], pb[t][:], ALU.add)
             nc.vector.tensor_tensor(dt[t][:].indirect(n4_t[:]), pa[t][:], nb[t][:], ALU.add)
 
-        def finish(t):
-            for h in range(2):
-                far = keep.tile([P, HALF], F32, name="far%d%d" % (t, h))
-                nc.scalar.activation(out=far[:], in_=dt[t][:].indirect(entries(n5_t, h)), func=ACT.Copy)
-                res = keep.tile([P, HALF], F32, name="res%d%d" % (t, h))
-                nc.vector.tensor_tensor(res[:], far[:], dt[t][:, cols(h)], ALU.max)
-                nc.sync.dma_start(out_rows[:, t, cols(h)], res[:])
+        def finish(t, halves):
+            for h in halves:
+                fetch(far[t][:, cols(h)], dt[t], entries(n5_t, cols(h)))
+            span = slice(halves[0] * HALF, (halves[-1] + 1) * HALF)
+            nc.vector.tensor_tensor(res[t][:, span], far[t][:, span], dt[t][:, span], ALU.max)
+            nc.sync.dma_start(out_rows[:, t, span], res[t][:, span])
 
-        product(0)
-        pair(0)
-        for t in range(PACK):
-            if t + 1 < PACK:
-                product(t + 1)
-                pair(t + 1)
-            put(t)
-            if t > 0:
-                finish(t - 1)
-        finish(PACK - 1)
+        for i, c in enumerate(CHUNKS):
+            ps = product(w2_ops[0], z_codes, z_scales, c, "bank%d" % i)
+            [nc.scalar.copy, nc.scalar.copy, nc.vector.tensor_copy][i](hid[0][:, c], ps[:])
+        first, second = slice(0, W // 2), slice(W // 2, W)
+        fetch(pa[0][:, first], hid[0], entries(n3_t, first))
+        nc.vector.tensor_copy(pb[0][:, first], hid[0][:].indirect(entries(n4_t, first)))
+        put_sum(0, first)
+        fetch(pa[0][:, second], hid[0], entries(n3_t, second))
+        fetch(pb[0][:, second], hid[0], entries(n4_t, second))
+        put_sum(0, second)
+        put_difference(0)
+        for t in range(1, PACK):
+            ps = product(w2_ops[t], z_codes, z_scales, whole, "bank%d" % (t + 2))
+            nc.scalar.copy(hid[t][:], ps[:])
+            fetch(pa[t][:], hid[t], n3_t[:])
+            fetch(pb[t][:], hid[t], n4_t[:])
+            put_sum(t, slice(0, W))
+            if t < PACK - 1:
+                finish(t - 1, [0, 1])
+            put_difference(t)
+        last = PACK - 1
+        quarter = slice(3 * S // 4, S)
+        nc.vector.tensor_copy(far[last][:, quarter], dt[last][:].indirect(entries(n5_t, quarter)))
+        finish(last - 1, [0, 1])
+        for span, done in ((cols(0), cols(0)), (slice(HALF, 3 * S // 4), cols(1))):
+            fetch(far[last][:, span], dt[last], entries(n5_t, span))
+            nc.vector.tensor_tensor(res[last][:, done], far[last][:, done], dt[last][:, done], ALU.max)
+            nc.sync.dma_start(out_rows[:, last, done], res[last][:, done])

@@ -42,9 +42,14 @@ def tile_picked_hashedbhaarh_none_p_kernel(
             return lst[:, span.start // 16 : span.stop // 16]
 
         def load_half(w, h, name, tag):
-            raw = keep.tile([P, PACK, HALF], F32, name=name, tag=tag)
+            raw = keep.tile([P, PACK, HALF], F32, name=name, tag=tag, align_bytes=64)
             nc.sync.dma_start(raw[:], w.rearrange("(p j) c -> p j c", j=PACK)[:, :, cols(h)])
             return raw
+
+        def load_rows(src, name, tag):
+            dst = keep.tile([P, PACK], F32, name=name, tag=tag, align_bytes=64)
+            nc.sync.dma_start(dst[:], src.rearrange("(p t) o -> p (t o)", t=PACK))
+            return dst
 
         def deal(engine_copy, grouped, raw, h):
             engine_copy(
@@ -86,21 +91,18 @@ def tile_picked_hashedbhaarh_none_p_kernel(
             nc.sync.dma_start(scale_table[e:P:16, :].bitcast(I32), x_scales[0, e:16:2].bitcast(I32))
         w1_raw = [load_half(w1, 0, "w1_raw0", "raw_a")]
         n1_t = load_list(n1, "n1_t")
-        n2_t = load_list(n2, "n2_t")
-        n3_t = load_list(n3, "n3_t")
+        sl_t = load_rows(sl, "sl_t", "sl_t")
+        th_t = load_rows(th, "th_t", "th_t")
         w1_raw.append(load_half(w1, 1, "w1_raw1", "raw_b"))
         word_table = keep.tile([P, T], I32, name="word_table")
         nc.sync.dma_start(word_table[:], x_words[0].rearrange("p n r -> p (n r)").bitcast(I32))
-        w2_raw = [load_half(w2, h, "w2_raw%d" % h, "raw_%s" % "cb"[h]) for h in range(1)]
+        w2_raw = [load_half(w2, 0, "w2_raw0", "raw_c")]
+        n2_t = load_list(n2, "n2_t")
+        n3_t = load_list(n3, "n3_t")
         n4_t = load_list(n4, "n4_t")
         n5_t = load_list(n5, "n5_t")
-        sl_t = keep.tile([P, PACK], F32, name="sl_t")
-        th_t = keep.tile([P, PACK], F32, name="th_t")
-        gn_t = keep.tile([P, PACK], F32, name="gn_t")
-        for dst, src in ((sl_t, sl), (th_t, th), (gn_t, gn)):
-            nc.gpsimd.dma_start(dst[:], src.rearrange("(p t) o -> p (t o)", t=PACK))
 
-        w1_grouped = keep.tile([P, PACK, P, PACK], BF16, name="w1_grouped", align_bytes=64)
+        w1_grouped = keep.tile([P, PACK, P, PACK], BF16, name="w1_grouped", tag="w1_grouped", align_bytes=64)
         deal(nc.scalar.copy, w1_grouped, w1_raw[0], 0)
         picked_scales = keep.tile([P, S], U8, name="picked_scales")
         nc.vector.tensor_copy(picked_scales[:], scale_table[:].indirect(offs_t[:]))
@@ -113,8 +115,8 @@ def tile_picked_hashedbhaarh_none_p_kernel(
             )
         deal(nc.vector.tensor_copy, w1_grouped, w1_raw[1], 1)
         w1_ops = quantize(w1_grouped, 0, 1, "w1_first") + quantize(w1_grouped, 1, PACK, "w1_rest")
-        w2_raw.append(load_half(w2, 1, "w2_raw1", "raw_b"))
 
+        gn_t = load_rows(gn, "gn_t", "w1_grouped")
         bias_t = keep.tile([P, PACK], F32, name="bias_t")
         nc.vector.scalar_tensor_tensor(bias_t[:], sl_t[:], -1.0, th_t[:], ALU.mult, ALU.mult)
         gain_t = keep.tile([P, PACK], F32, name="gain_t")
@@ -122,13 +124,16 @@ def tile_picked_hashedbhaarh_none_p_kernel(
 
         picked = keep.tile([P, S], U32, name="picked_words", align_bytes=64)
         y = [keep.tile([P, S], F32, name="y%d" % t) for t in range(PACK)]
-        sg = [keep.tile([P, S], F32, name="sg%d" % t) for t in range(PACK)]
+        sg = [keep.tile([P, S], F32, name="sg%d" % t, tag="sg%d" % t) for t in range(PACK)]
         for h in range(2):
             nc.vector.tensor_copy(picked[:, cols(h)], word_table[:].bitcast(U32).indirect(entries(offs_t, cols(h))))
-        for t in range(PACK):
-            for h in range(2):
-                ps = product(w1_ops[t], picked, x_plane, cols(h), "bank%d" % (2 * t + h))
-                [[nc.scalar.copy, nc.scalar.copy, nc.scalar.copy, nc.vector.tensor_copy], [nc.vector.tensor_copy, nc.vector.tensor_copy, nc.vector.tensor_copy, nc.vector.tensor_copy]][h][t](y[t][:, cols(h)], ps[:])
+        for h in range(2):
+            ps = product(w1_ops[0], picked, x_plane, cols(h), "bank%d" % h)
+            nc.vector.tensor_copy(y[0][:, cols(h)], ps[:])
+        for t in range(1, PACK):
+            ps = product(w1_ops[t], picked, x_plane, whole, "bank%d" % (t + 5 - 1))
+            nc.vector.tensor_copy(y[t][:], ps[:])
+        w2_raw.append(load_half(w2, 1, "w2_raw1", "w1_rest"))
         w2_grouped = keep.tile([P, PACK, P, PACK], BF16, name="w2_grouped", align_bytes=64)
         for t in range(PACK):
             for h in range(2):
@@ -143,7 +148,7 @@ def tile_picked_hashedbhaarh_none_p_kernel(
         z_head = keep.tile([P, PACK, HALF], BF16, name="z_head")
         z_tail = keep.tile([P, 2, PACK, HALF // 2], BF16, name="z_tail")
         z_planes = [z_head[:], z_tail[:, 0], z_tail[:, 1]]
-        diff = [keep.tile([P, S], F32, name="diff%d" % t) for t in range(PACK)]
+        diff = [keep.tile([P, S], F32, name="diff%d" % t) for t in range(OWN)]
 
         def scale_diff(dst, t, c, pattern=None):
             d, v = diff[t][:, c], y[t][:, c]
@@ -159,8 +164,6 @@ def tile_picked_hashedbhaarh_none_p_kernel(
 
         twin = copy_of(0)
         deal(nc.vector.tensor_copy, w2_grouped, w2_raw[0], 0)
-        deal(nc.vector.tensor_copy, w2_grouped, w2_raw[1], 1)
-        w2_ops = quantize(w2_grouped, 0, 1, "w2_first")
         for t in range(OWN):
             for h in range(2):
                 nc.vector.tensor_tensor(
@@ -170,48 +173,64 @@ def tile_picked_hashedbhaarh_none_p_kernel(
                 twin = copy_of(t + 1)
             scale_diff(z_head[:, t, :], t, cols(0))
             scale_diff(z_tail[:, :, t, :], t, cols(1), "p (u c) -> p u c")
+        diff.append(keep.tile([P, S], F32, name="diff2", tag="twin"))
+        diff.append(keep.tile([P, S], F32, name="diff3", tag="sg1"))
         z_codes = keep.tile([P, S], U32, name="z_codes", align_bytes=64)
         z_scales = keep.tile([P, S], U8, name="z_scales", align_bytes=64)
         fetched = {t: keep.tile([P, S], F32, name="fetched%d" % t) for t in range(OWN, PACK)}
-        z_grouped = keep.tile([P, S, PACK], BF16, name="z_grouped", tag="late", align_bytes=64)
+        z_grouped = [
+            keep.tile([P, c.stop - c.start, PACK], BF16, name="z_grouped%d" % i, tag="grouped%d" % i, align_bytes=64)
+            for i, c in enumerate(CHUNKS)
+        ]
 
-        def quantize_z(c):
+        def quantize_z(i):
+            c = CHUNKS[i]
             nc.vector.quantize_mx(
-                out=z_codes[:, c].bitcast(FP8X4), scales=z_scales[:, c], in_=z_grouped[:, c].rearrange("p s t -> p (s t)")
+                out=z_codes[:, c].bitcast(FP8X4), scales=z_scales[:, c], in_=z_grouped[i][:].rearrange("p s t -> p (s t)")
             )
 
-        for i, c in enumerate(CHUNKS):
+        for c in CHUNKS:
             for t in range(OWN, PACK):
                 fetch(fetched[t][:, c], sg[t], entries(n2_t, c))
+        deal(nc.scalar.copy, w2_grouped, w2_raw[1], 1)
+        for i, c in enumerate(CHUNKS):
+            for t in range(OWN, PACK):
                 nc.vector.tensor_tensor(diff[t][:, c], fetched[t][:, c], sg[t][:, c], ALU.subtract)
             for t in range(OWN, PACK):
                 scale_diff(z_planes[i][:, t, :], t, c)
 
             if i == 2:
-                quantize_z(CHUNKS[0])
+                w2_ops = quantize(w2_grouped, 0, 1, "w2_first")
             [nc.scalar.copy, nc.scalar.copy, nc.vector.tensor_copy][i](
-                z_grouped[:, c].rearrange("p (c i) t -> p c t i", i=4),
+                z_grouped[i][:].rearrange("p (c i) t -> p c t i", i=4),
                 z_planes[i].rearrange("p t (c i) -> p c t i", i=4),
             )
-        for c in CHUNKS[1:]:
-            quantize_z(c)
+        for i in (0, 1, 2):
+            quantize_z(i)
 
 
-        w2_ops = w2_ops + quantize(w2_grouped, 1, PACK, "w2_rest", "late")
+        w2_ops = w2_ops + quantize(w2_grouped, 1, PACK, "w2_rest", "grouped2")
         out_rows = out.rearrange("(p t) s -> p t s", t=PACK)
-        hid = [keep.tile([P, S], F32, name="hid%d" % t) for t in range(PACK)]
-        pa = [keep.tile([P, W], F32, name="pa%d" % t) for t in range(PACK)]
-        pb = [keep.tile([P, W], F32, name="pb%d" % t) for t in range(PACK)]
-        nb = [keep.tile([P, W], F32, name="nb%d" % t) for t in range(PACK)]
-        dt = [keep.tile([P, S], F32, name="dt%d" % t) for t in range(PACK)]
-        far = [keep.tile([P, S], F32, name="far%d" % t) for t in range(PACK)]
-        res = [keep.tile([P, S], F32, name="res%d" % t) for t in range(PACK)]
+        hid, pa, pb, nb, dt, far, res = {}, {}, {}, {}, {}, {}, {}
+
+        def start_tile(t):
+            hid[t] = keep.tile([P, S], F32, name="hid%d" % t, tag="hid%d" % t)
+            pa[t] = keep.tile([P, W], F32, name="pa%d" % t)
+            pb[t] = keep.tile([P, W], F32, name="pb%d" % t, tag="pb%d" % t)
+            nb[t] = keep.tile([P, W], F32, name="nb%d" % t, tag="nb%d" % t)
+            dt[t] = keep.tile([P, S], F32, name="dt%d" % t, tag="dt%d" % t)
+
+        def end_tile(t):
+            far[t] = keep.tile([P, S], F32, name="far%d" % t, tag="hid%d" % (t + 1))
+            res[t] = keep.tile([P, S], F32, name="res%d" % t)
+
+        def negate(t):
+            nc.scalar.activation(out=nb[t][:], in_=pb[t][:], func=ACT.Copy, scale=-1.0)
 
         def put_sum(t, span):
             nc.vector.tensor_tensor(dt[t][:].indirect(entries(n3_t, span)), pa[t][:, span], pb[t][:, span], ALU.add)
 
         def put_difference(t):
-            nc.scalar.activation(out=nb[t][:], in_=pb[t][:], func=ACT.Copy, scale=-1.0)
             nc.vector.tensor_tensor(dt[t][:].indirect(n4_t[:]), pa[t][:], nb[t][:], ALU.add)
 
         def finish(t, halves):
@@ -221,6 +240,7 @@ def tile_picked_hashedbhaarh_none_p_kernel(
             nc.vector.tensor_tensor(res[t][:, span], far[t][:, span], dt[t][:, span], ALU.max)
             nc.sync.dma_start(out_rows[:, t, span], res[t][:, span])
 
+        start_tile(0)
         for i, c in enumerate(CHUNKS):
             ps = product(w2_ops[0], z_codes, z_scales, c, "bank%d" % i)
             [nc.scalar.copy, nc.scalar.copy, nc.vector.tensor_copy][i](hid[0][:, c], ps[:])
@@ -231,17 +251,22 @@ def tile_picked_hashedbhaarh_none_p_kernel(
         fetch(pa[0][:, second], hid[0], entries(n3_t, second))
         fetch(pb[0][:, second], hid[0], entries(n4_t, second))
         put_sum(0, second)
+        negate(0)
         put_difference(0)
         for t in range(1, PACK):
+            start_tile(t)
             ps = product(w2_ops[t], z_codes, z_scales, whole, "bank%d" % (t + 2))
             nc.scalar.copy(hid[t][:], ps[:])
             fetch(pa[t][:], hid[t], n3_t[:])
             fetch(pb[t][:], hid[t], n4_t[:])
             put_sum(t, slice(0, W))
+            end_tile(t - 1)
             if t < PACK - 1:
                 finish(t - 1, [0, 1])
+            negate(t)
             put_difference(t)
         last = PACK - 1
+        end_tile(last)
         quarter = slice(3 * S // 4, S)
         nc.vector.tensor_copy(far[last][:, quarter], dt[last][:].indirect(entries(n5_t, quarter)))
         finish(last - 1, [0, 1])

@@ -96,7 +96,7 @@ def tile_picked_hashedbhaarh_none_p_kernel(
         w1_raw.append(load_half(w1, 1, "w1_raw1", "raw_b"))
         word_table = keep.tile([P, T], I32, name="word_table")
         nc.sync.dma_start(word_table[:], x_words[0].rearrange("p n r -> p (n r)").bitcast(I32))
-        w2_raw = [load_half(w2, 0, "w2_raw0", "raw_c")]
+        gn_t = load_rows(gn, "gn_t", "gn_t")
         n2_t = load_list(n2, "n2_t")
         n3_t = load_list(n3, "n3_t")
         n4_t = load_list(n4, "n4_t")
@@ -116,7 +116,7 @@ def tile_picked_hashedbhaarh_none_p_kernel(
         deal(nc.vector.tensor_copy, w1_grouped, w1_raw[1], 1)
         w1_ops = quantize(w1_grouped, 0, 1, "w1_first") + quantize(w1_grouped, 1, PACK, "w1_rest")
 
-        gn_t = load_rows(gn, "gn_t", "w1_grouped")
+        w2_raw = [load_half(w2, 0, "w2_raw0", "raw_b")]
         bias_t = keep.tile([P, PACK], F32, name="bias_t")
         nc.vector.scalar_tensor_tensor(bias_t[:], sl_t[:], -1.0, th_t[:], ALU.mult, ALU.mult)
         gain_t = keep.tile([P, PACK], F32, name="gain_t")
@@ -127,12 +127,10 @@ def tile_picked_hashedbhaarh_none_p_kernel(
         sg = [keep.tile([P, S], F32, name="sg%d" % t, tag="sg%d" % t) for t in range(PACK)]
         for h in range(2):
             nc.vector.tensor_copy(picked[:, cols(h)], word_table[:].bitcast(U32).indirect(entries(offs_t, cols(h))))
-        for h in range(2):
-            ps = product(w1_ops[0], picked, x_plane, cols(h), "bank%d" % h)
-            nc.vector.tensor_copy(y[0][:, cols(h)], ps[:])
-        for t in range(1, PACK):
-            ps = product(w1_ops[t], picked, x_plane, whole, "bank%d" % (t + 5 - 1))
-            nc.vector.tensor_copy(y[t][:], ps[:])
+        for t in range(PACK):
+            for h, span in enumerate((cols(0), cols(1)) if t < 2 else (whole,)):
+                ps = product(w1_ops[t], picked, x_plane, span, "bank%d" % (2 * t + h))
+                nc.vector.tensor_copy(y[t][:, span], ps[:])
         w2_raw.append(load_half(w2, 1, "w2_raw1", "w1_rest"))
         w2_grouped = keep.tile([P, PACK, P, PACK], BF16, name="w2_grouped", align_bytes=64)
         for t in range(PACK):

from contextlib import ExitStack

import concourse.mybir as mybir

F32 = mybir.dt.float32
BF16 = mybir.dt.bfloat16
I32 = mybir.dt.int32
U32 = mybir.dt.uint32
U16 = mybir.dt.uint16
U8 = mybir.dt.uint8
FP8X4 = mybir.dt.float8_e4m3fn_x4
ALU = mybir.AluOpType
ACT = mybir.ActivationFunctionType

P = 128
PACK = 4
K, T, S, H, N, W = 512, 2048, 512, 512, 512, 256
HALF = S // 2
FLOPS = 2 * K * H * S + 2 * H * N * S
CHUNKS = [slice(0, 256), slice(256, 384), slice(384, 512)]
OWN = 2


def tile_picked_hashedbhaarh_none_p_kernel(
    tc, x_words, x_scales, w1, sl, th, gn, w2, offs, n1, n2, n3, n4, n5, out
):
    nc = tc.nc
    with ExitStack() as ctx:
        lists = ctx.enter_context(tc.tile_pool(name="lists", bufs=1))
        keep = ctx.enter_context(tc.tile_pool(name="keep", bufs=1))
        psum = ctx.enter_context(tc.psum_pool(name="psum", bufs=1))

        def load_list(src, name):
            t = lists.tile(list(src.shape), U16, name=name)
            nc.sync.dma_start(t[:], src)
            return t

        def cols(h):
            return slice(h * HALF, (h + 1) * HALF)

        def entries(lst, span):
            return lst[:, span.start // 16 : span.stop // 16]

        def load_half(w, h, name, tag):
            raw = keep.tile([P, PACK, HALF], F32, name=name, tag=tag, align_bytes=64)
            nc.sync.dma_start(raw[:], w.rearrange("(p j) c -> p j c", j=PACK)[:, :, cols(h)])
            return raw

        def load_rows(src, name, tag):
            dst = keep.tile([P, PACK], F32, name=name, tag=tag, align_bytes=64)
            nc.sync.dma_start(dst[:], src.rearrange("(p t) o -> p (t o)", t=PACK))
            return dst

        def deal(engine_copy, grouped, raw, h):
            engine_copy(
                grouped[:, :, h * 64 : (h + 1) * 64, :].rearrange("p t m j -> p m j t"),
                raw[:].rearrange("p j (m t) -> p m j t", t=PACK),
            )

        def quantize(grouped, t0, t1, name, tag=None):
            width = (t1 - t0) * P
            codes = keep.tile([P, width], U32, name=name + "_codes", tag=tag or name, align_bytes=64)
            scales = keep.tile([P, width], U8, name=name + "_scales", align_bytes=64)
            nc.vector.quantize_mx(
                out=codes[:].bitcast(FP8X4), scales=scales[:], in_=grouped[:, t0:t1].rearrange("p t m j -> p (t m j)")
            )
            return [(codes[:, i * P : (i + 1) * P], scales[:, i * P : (i + 1) * P]) for i in range(t1 - t0)]

        def product(weights, moving, moving_scales, span, tag):
            ps = psum.tile([P, span.stop - span.start], F32, name="ps_" + tag, tag=tag)
            nc.tensor.matmul_mx(
                out=ps[:],
                lhsT=weights[0].bitcast(FP8X4),
                lhsT_scale=weights[1],
                rhs=moving[:, span].bitcast(FP8X4),
                rhs_scale=moving_scales[:, span],
                start=True,
                stop=True,
            )
            return ps

        def fetch(dst, window, offsets):
            nc.scalar.activation(out=dst, in_=window[:].indirect(offsets), func=ACT.Copy)

        whole = slice(0, S)

        scale_table = keep.tile([P, T], U8, name="scale_table")
        nc.gpsimd.memset(scale_table[:].bitcast(I32), 0)
        offs_t = load_list(offs, "offs_t")
        for e in range(2):
            nc.sync.dma_start(scale_table[e:P:16, :].bitcast(I32), x_scales[0, e:16:2].bitcast(I32))
        w1_raw = [load_half(w1, 0, "w1_raw0", "raw_a")]
        n1_t = load_list(n1, "n1_t")
        sl_t = load_rows(sl, "sl_t", "sl_t")
        th_t = load_rows(th, "th_t", "th_t")
        w1_raw.append(load_half(w1, 1, "w1_raw1", "raw_b"))
        word_table = keep.tile([P, T], I32, name="word_table")
        nc.sync.dma_start(word_table[:], x_words[0].rearrange("p n r -> p (n r)").bitcast(I32))
        gn_t = load_rows(gn, "gn_t", "gn_t")
        n2_t = load_list(n2, "n2_t")
        n3_t = load_list(n3, "n3_t")
        n4_t = load_list(n4, "n4_t")
        n5_t = load_list(n5, "n5_t")

        w1_grouped = keep.tile([P, PACK, P, PACK], BF16, name="w1_grouped", tag="w1_grouped", align_bytes=64)
        deal(nc.scalar.copy, w1_grouped, w1_raw[0], 0)
        picked_scales = keep.tile([P, S], U8, name="picked_scales")
        nc.vector.tensor_copy(picked_scales[:], scale_table[:].indirect(offs_t[:]))
        x_plane = keep.tile([P, S], U8, name="x_plane", align_bytes=64)
        nc.vector.tensor_copy(x_plane[:].bitcast(I32), picked_scales[:].bitcast(I32))
        for e in range(2):
            nc.scalar.dma_start(
                x_plane[2 + e : P : 32, :].bitcast(I32),
                picked_scales[16 + e : P : 32, :].bitcast(I32),
            )
        deal(nc.vector.tensor_copy, w1_grouped, w1_raw[1], 1)
        w1_ops = quantize(w1_grouped, 0, 1, "w1_first") + quantize(w1_grouped, 1, PACK, "w1_rest")

        w2_raw = [load_half(w2, 0, "w2_raw0", "raw_b")]
        bias_t = keep.tile([P, PACK], F32, name="bias_t")
        nc.vector.scalar_tensor_tensor(bias_t[:], sl_t[:], -1.0, th_t[:], ALU.mult, ALU.mult)
        gain_t = keep.tile([P, PACK], F32, name="gain_t")
        nc.vector.tensor_scalar(gain_t[:], gn_t[:], -1.5, None, ALU.mult)

        picked = keep.tile([P, S], U32, name="picked_words", align_bytes=64)
        y = [keep.tile([P, S], F32, name="y%d" % t) for t in range(PACK)]
        sg = [keep.tile([P, S], F32, name="sg%d" % t, tag="sg%d" % t) for t in range(PACK)]
        for h in range(2):
            nc.vector.tensor_copy(picked[:, cols(h)], word_table[:].bitcast(U32).indirect(entries(offs_t, cols(h))))
        for t in range(PACK):
            for h, span in enumerate((cols(0), cols(1)) if t < 2 else (whole,)):
                ps = product(w1_ops[t], picked, x_plane, span, "bank%d" % (2 * t + h))
                nc.vector.tensor_copy(y[t][:, span], ps[:])
        w2_raw.append(load_half(w2, 1, "w2_raw1", "w1_rest"))
        w2_grouped = keep.tile([P, PACK, P, PACK], BF16, name="w2_grouped", align_bytes=64)
        for t in range(PACK):
            for h in range(2):
                nc.scalar.activation(
                    out=sg[t][:, cols(h)],
                    in_=y[t][:].indirect(entries(n1_t, cols(h))),
                    func=ACT.Sigmoid,
                    scale=sl_t[:, t : t + 1],
                    bias=bias_t[:, t : t + 1],
                )

        z_head = keep.tile([P, PACK, HALF], BF16, name="z_head")
        z_tail = keep.tile([P, 2, PACK, HALF // 2], BF16, name="z_tail")
        z_planes = [z_head[:], z_tail[:, 0], z_tail[:, 1]]
        diff = [keep.tile([P, S], F32, name="diff%d" % t) for t in range(OWN)]

        def scale_diff(dst, t, c, pattern=None):
            d, v = diff[t][:, c], y[t][:, c]
            if pattern:
                d, v = d.rearrange(pattern, u=2), v.rearrange(pattern, u=2)
            nc.vector.scalar_tensor_tensor(dst, d, gain_t[:, t : t + 1], v, ALU.mult, ALU.mult)


        def copy_of(t):
            twin = keep.tile([P, S], F32, name="sg_twin%d" % t, tag="twin")
            nc.vector.tensor_copy(twin[:], sg[t][:])
            return twin

        twin = copy_of(0)
        deal(nc.vector.tensor_copy, w2_grouped, w2_raw[0], 0)
        for t in range(OWN):
            for h in range(2):
                nc.vector.tensor_tensor(
                    diff[t][:, cols(h)], sg[t][:].indirect(entries(n2_t, cols(h))), twin[:, cols(h)], ALU.subtract
                )
            if t + 1 < OWN:
                twin = copy_of(t + 1)
            scale_diff(z_head[:, t, :], t, cols(0))
            scale_diff(z_tail[:, :, t, :], t, cols(1), "p (u c) -> p u c")
        diff.append(keep.tile([P, S], F32, name="diff2", tag="twin"))
        diff.append(keep.tile([P, S], F32, name="diff3", tag="sg1"))
        z_codes = keep.tile([P, S], U32, name="z_codes", align_bytes=64)
        z_scales = keep.tile([P, S], U8, name="z_scales", align_bytes=64)
        fetched = {t: keep.tile([P, S], F32, name="fetched%d" % t) for t in range(OWN, PACK)}
        z_grouped = [
            keep.tile([P, c.stop - c.start, PACK], BF16, name="z_grouped%d" % i, tag="grouped%d" % i, align_bytes=64)
            for i, c in enumerate(CHUNKS)
        ]

        def quantize_z(i):
            c = CHUNKS[i]
            nc.vector.quantize_mx(
                out=z_codes[:, c].bitcast(FP8X4), scales=z_scales[:, c], in_=z_grouped[i][:].rearrange("p s t -> p (s t)")
            )

        for c in CHUNKS:
            for t in range(OWN, PACK):
                fetch(fetched[t][:, c], sg[t], entries(n2_t, c))
        deal(nc.scalar.copy, w2_grouped, w2_raw[1], 1)
        for i, c in enumerate(CHUNKS):
            for t in range(OWN, PACK):
                nc.vector.tensor_tensor(diff[t][:, c], fetched[t][:, c], sg[t][:, c], ALU.subtract)
            for t in range(OWN, PACK):
                scale_diff(z_planes[i][:, t, :], t, c)

            if i == 2:
                w2_ops = quantize(w2_grouped, 0, 1, "w2_first")
            [nc.scalar.copy, nc.scalar.copy, nc.vector.tensor_copy][i](
                z_grouped[i][:].rearrange("p (c i) t -> p c t i", i=4),
                z_planes[i].rearrange("p t (c i) -> p c t i", i=4),
            )
        for i in (0, 1, 2):
            quantize_z(i)


        w2_ops = w2_ops + quantize(w2_grouped, 1, PACK, "w2_rest", "grouped2")
        out_rows = out.rearrange("(p t) s -> p t s", t=PACK)
        hid, pa, pb, nb, dt, far, res = {}, {}, {}, {}, {}, {}, {}

        def start_tile(t):
            hid[t] = keep.tile([P, S], F32, name="hid%d" % t, tag="hid%d" % t)
            pa[t] = keep.tile([P, W], F32, name="pa%d" % t)
            pb[t] = keep.tile([P, W], F32, name="pb%d" % t, tag="pb%d" % t)
            nb[t] = keep.tile([P, W], F32, name="nb%d" % t, tag="nb%d" % t)
            dt[t] = keep.tile([P, S], F32, name="dt%d" % t, tag="dt%d" % t)

        def end_tile(t):
            far[t] = keep.tile([P, S], F32, name="far%d" % t, tag="hid%d" % (t + 1))
            res[t] = keep.tile([P, S], F32, name="res%d" % t)

        def negate(t):
            nc.scalar.activation(out=nb[t][:], in_=pb[t][:], func=ACT.Copy, scale=-1.0)

        def put_sum(t, span):
            nc.vector.tensor_tensor(dt[t][:].indirect(entries(n3_t, span)), pa[t][:, span], pb[t][:, span], ALU.add)

        def put_difference(t):
            nc.vector.tensor_tensor(dt[t][:].indirect(n4_t[:]), pa[t][:], nb[t][:], ALU.add)

        def finish(t, halves):
            for h in halves:
                fetch(far[t][:, cols(h)], dt[t], entries(n5_t, cols(h)))
            span = slice(halves[0] * HALF, (halves[-1] + 1) * HALF)
            nc.vector.tensor_tensor(res[t][:, span], far[t][:, span], dt[t][:, span], ALU.max)
            nc.sync.dma_start(out_rows[:, t, span], res[t][:, span])

        start_tile(0)
        for i, c in enumerate(CHUNKS):
            ps = product(w2_ops[0], z_codes, z_scales, c, "bank%d" % i)
            [nc.scalar.copy, nc.scalar.copy, nc.vector.tensor_copy][i](hid[0][:, c], ps[:])
        first, second = slice(0, W // 2), slice(W // 2, W)
        fetch(pa[0][:, first], hid[0], entries(n3_t, first))
        nc.vector.tensor_copy(pb[0][:, first], hid[0][:].indirect(entries(n4_t, first)))
        put_sum(0, first)
        fetch(pa[0][:, second], hid[0], entries(n3_t, second))
        fetch(pb[0][:, second], hid[0], entries(n4_t, second))
        put_sum(0, second)
        negate(0)
        put_difference(0)
        for t in range(1, PACK):
            start_tile(t)
            ps = product(w2_ops[t], z_codes, z_scales, whole, "bank%d" % (t + 2))
            nc.scalar.copy(hid[t][:], ps[:])
            fetch(pa[t][:], hid[t], n3_t[:])
            fetch(pb[t][:], hid[t], n4_t[:])
            put_sum(t, slice(0, W))
            end_tile(t - 1)
            if t < PACK - 1:
                finish(t - 1, [0, 1])
            negate(t)
            put_difference(t)
        last = PACK - 1
        end_tile(last)
        quarter = slice(3 * S // 4, S)
        nc.vector.tensor_copy(far[last][:, quarter], dt[last][:].indirect(entries(n5_t, quarter)))
        finish(last - 1, [0, 1])
        for span, done in ((cols(0), cols(0)), (slice(HALF, 3 * S // 4), cols(1))):
            fetch(far[last][:, span], dt[last], entries(n5_t, span))
            nc.vector.tensor_tensor(res[last][:, done], far[last][:, done], dt[last][:, done], ALU.max)
            nc.sync.dma_start(out_rows[:, last, done], res[last][:, done])
